import numpy as np
import ml_dtypes


def mxq(x, axis, fmt="e4m3"):
    dtype, down = {"e4m3": (ml_dtypes.float8_e4m3fn, 7), "e5m2": (ml_dtypes.float8_e5m2, 14)}[fmt]
    v = np.moveaxis(np.asarray(x, np.float32).astype(ml_dtypes.bfloat16).astype(np.float64), axis, -1)
    blocks = v.reshape(v.shape[:-1] + (-1, 32))
    amax = np.abs(blocks).max(-1, keepdims=True)
    byte = np.maximum(np.where(amax > 0, np.frexp(amax)[1] - 1 + 127, 0) - down, 1)
    scale = np.exp2(byte - 127.0)
    codes = (blocks / scale).astype(np.float32).astype(dtype).astype(np.float64)
    return np.moveaxis((codes * scale).reshape(v.shape), -1, axis)


WIDE = False


def mx_kscale(k):
    if not WIDE:
        return np.ones(k)
    levels = np.array([10, -10, 5, -5, 0])
    if k % 512:
        return np.exp2(np.random.permutation(np.resize(levels, k // 32))).repeat(32)
    a = np.empty((k // 512, 16))
    for p in range(k // 512):
        a[p, :8] = np.random.permutation(np.resize(levels, 8))
        for g in range(8):
            far = levels[np.abs(levels - a[p, g]) >= 10]
            a[p, g + 8] = far[np.random.randint(len(far))]
    return np.exp2(a.ravel()).repeat(32)


def f64(x):
    return np.asarray(x).astype(np.float64)


def striped(idx):
    return np.tile(idx.reshape(-1, 16).T, (8, 1)).astype(np.uint16)


def unstriped(offs):
    return offs[:16].T.reshape(-1).astype(np.int64)


def striped8(idx):
    return np.concatenate([x.reshape(-1, 16).T for x in idx]).astype(np.uint16)


def runs(offs, k):
    lists = np.stack([offs[16 * r : 16 * r + 16].T.reshape(-1) for r in range(8)]).astype(np.int64)
    return lists[np.arange(k) % 512 // 64]


def pack_weight(w):
    k, n = w.shape
    w = f64(np.asarray(w, np.float32).astype(ml_dtypes.bfloat16)).reshape(k // 32, 32, n)
    amax = np.abs(w).max(1)
    byte = np.clip(np.where(amax > 0, np.frexp(amax)[1] - 1 + 127 - 7, 1), 1, 254)
    scaled = (w * np.exp2(127.0 - byte)[:, None, :]).reshape(k, n).astype(np.float32)
    words = np.ascontiguousarray(scaled.reshape(k // 512, 128, 4, n).transpose(0, 1, 3, 2)).astype(ml_dtypes.float8_e4m3fn).view(np.uint8)
    return words, np.ascontiguousarray(byte.astype(np.uint8).reshape(k // 512, 16, n))


def unpack_weight(words, scales):
    g, p, n, _ = words.shape
    vals = np.ascontiguousarray(words).view(ml_dtypes.float8_e4m3fn).astype(np.float64) * np.repeat(np.exp2(scales.astype(np.float64) - 127.0), 8, axis=1)[..., None]
    return vals.transpose(0, 1, 3, 2).reshape(g * 512, n)


def sigmoid(v):
    return 1.0 / (1.0 + np.exp(-np.maximum(v, -700.0)))


K, T, S, V, N, G, H = 512, 2048, 512, 256, 512, 2048, 512


def setup_inputs():
    n = np.random.standard_normal
    s = mx_kscale(K)[:, None]
    u = mx_kscale(S)
    packed_xT = pack_weight(n((K, T)) * s)
    packed_dT = pack_weight(n((K, G)) / s)
    return {
        "x_words": packed_xT[0],
        "x_scales": packed_xT[1],
        "d_words": packed_dT[0],
        "d_scales": packed_dT[1],
        "gn": (np.random.uniform(0.5, 1.5, (H, 1)) * u[:, None]).astype(np.float32),
        "w1": (n((H, N)) / np.sqrt(H) / u[:, None]).astype(np.float32),
        "offs": striped8(np.random.randint(0, T, (8, S))),
        "k1": striped8(np.random.randint(0, G, (8, H))),
        "n1": striped(np.random.permutation(S)),
        "n2": striped(np.random.permutation(V)),
        "n3": striped(np.random.permutation(V)),
    }


def reference(x_words, x_scales, d_words, d_scales, gn, w1, offs, k1, n1, n2, n3):
    d_k1 = unpack_weight(d_words, d_scales)[np.arange(K)[:, None], runs(k1, K)]
    xq = unpack_weight(x_words, x_scales)[np.arange(K)[:, None], runs(offs, K)]
    h = 0.0625 * (d_k1.T @ xq)
    ln = h[:, unstriped(n1)]
    sq = (ln) ** 2
    ms = sq.reshape(H, V, 2).sum(axis=2)
    z = f64(gn) * np.sqrt(ms + 0.1)
    h2 = mxq(f64(w1), 0, "e4m3").T @ mxq(z, 0, "e4m3")
    return h2 + (sigmoid(h2[:, unstriped(n2)])) * (h2[:, unstriped(n3)] - h2)

@@ -1,0 +1,216 @@
+from contextlib import ExitStack
+
+import concourse.mybir as mybir
+
+F32 = mybir.dt.float32
+BF16 = mybir.dt.bfloat16
+I32 = mybir.dt.int32
+U32 = mybir.dt.uint32
+U16 = mybir.dt.uint16
+U8 = mybir.dt.uint8
+FP8X4 = mybir.dt.float8_e4m3fn_x4
+ACT = mybir.ActivationFunctionType
+ALU = mybir.AluOpType
+
+P = 128
+PACK = 4
+K, T, S, V, N, G, H = 512, 2048, 512, 256, 512, 2048, 512
+FLOPS = 2 * K * H * S + 2 * H * N * V
+
+
+def tile_picked_hpqhprmstrack_none_p_kernel(
+    tc, x_words, x_scales, d_words, d_scales, gn, w1, offs, k1, n1, n2, n3, out
+):
+    nc = tc.nc
+    with ExitStack() as ctx:
+        lists = ctx.enter_context(tc.tile_pool(name="lists", bufs=1))
+        sb = ctx.enter_context(tc.tile_pool(name="sb", bufs=1))
+        psum = ctx.enter_context(tc.psum_pool(name="psum", bufs=1))
+
+        def load_list(src, name):
+            held = lists.tile(list(src.shape), U16, name=name)
+            nc.sync.dma_start(held[:], src)
+            return held
+
+        def tile(shape, dtype, name):
+            return sb.tile(shape, dtype, name=name, align_bytes=64)
+
+        d_bytes_tab = tile([P, G], U8, "d_bytes_tab")
+        x_bytes_tab = tile([P, T], U8, "x_bytes_tab")
+        plane = tile([P, H + S], U8, "plane")
+        nc.vector.memset(d_bytes_tab[:].bitcast(I32), 0)
+        nc.vector.memset(x_bytes_tab[:].bitcast(I32), 0)
+        nc.vector.memset(plane[:].bitcast(I32), 0)
+
+        k1_t = load_list(k1, "k1_t")
+        offs_t = load_list(offs, "offs_t")
+        d_tab = tile([P, G], U32, "d_tab")
+        nc.sync.dma_start(d_tab[:].bitcast(I32), d_words[0].rearrange("p n t -> p (n t)").bitcast(I32))
+        nc.scalar.dma_start(d_bytes_tab[0:P:8, :].bitcast(I32), d_scales[0].bitcast(I32))
+        nc.scalar.dma_start(x_bytes_tab[0:P:8, :].bitcast(I32), x_scales[0].bitcast(I32))
+        n1_t = load_list(n1, "n1_t")
+        n2_t = load_list(n2, "n2_t")
+        n3_t = load_list(n3, "n3_t")
+        x_tab = tile([P, T], U32, "x_tab")
+        nc.sync.dma_start(x_tab[:].bitcast(I32), x_words[0].rearrange("p n t -> p (n t)").bitcast(I32))
+        gn_t = tile([P, PACK], F32, "gn_t")
+        nc.gpsimd.dma_start(gn_t[:], gn.rearrange("(p t) o -> p (t o)", t=PACK))
+        w_view = w1.rearrange("(p j) m -> p j m", j=PACK)
+        w_raw = []
+        for c in range(2):
+            raw = tile([P, PACK, N // 2], F32, "w_raw%d" % c)
+            nc.sync.dma_start(raw[:], w_view[:, :, c * (N // 2) : (c + 1) * (N // 2)])
+            w_raw.append(raw)
+
+        got_bytes = tile([P, H + S], U8, "got_bytes")
+        nc.vector.tensor_copy(got_bytes[:, 0:H], d_bytes_tab[:].indirect(k1_t[:]))
+        nc.vector.tensor_copy(got_bytes[:, H : H + S], x_bytes_tab[:].indirect(offs_t[:]))
+        dealt_bytes = tile([P, H + S], U8, "dealt_bytes")
+        nc.vector.tensor_copy(
+            dealt_bytes[:, 0:H].rearrange("p (t m) -> p t m", t=PACK),
+            got_bytes[:, 0:H].rearrange("p (m t) -> p t m", t=PACK),
+        )
+        nc.vector.tensor_copy(dealt_bytes[:, H : H + S].bitcast(I32), got_bytes[:, H : H + S].bitcast(I32))
+        for j in range(4):
+            nc.scalar.dma_start(plane[j:P:32, :].bitcast(I32), dealt_bytes[8 * j : P : 32, :].bitcast(I32))
+
+        d_got = tile([P, H], U32, "d_got")
+        nc.vector.tensor_copy(d_got[:], d_tab[:].indirect(k1_t[:]))
+        d_dealt = tile([P, H], U32, "d_dealt")
+        nc.vector.tensor_copy(
+            d_dealt[:].rearrange("p (t c i) -> p c t i", t=PACK, i=4),
+            d_got[:].rearrange("p (c i t) -> p c t i", t=PACK, i=4),
+        )
+        x_got = tile([P, S], U32, "x_got")
+        nc.vector.tensor_copy(x_got[:], x_tab[:].indirect(offs_t[:]))
+
+        sq = []
+        for t in range(PACK):
+            bank = psum.tile([P, S], F32, name="h_bank%d" % t)
+            cols = slice(t * P, (t + 1) * P)
+            nc.tensor.matmul_mx(
+                out=bank[:],
+                lhsT=d_dealt[:, cols].bitcast(FP8X4),
+                lhsT_scale=plane[:, cols],
+                rhs=x_got[:].bitcast(FP8X4),
+                rhs_scale=plane[:, H : H + S],
+                start=True,
+                stop=True,
+            )
+            sq_t = tile([P, S], F32, "sq%d" % t)
+            nc.scalar.activation(out=sq_t[:], in_=bank[:], func=ACT.Square, scale=0.0625)
+            sq.append(sq_t)
+
+        w_codes = tile([P, N], U32, "w_codes")
+        w_plane = tile([P, N], U8, "w_plane")
+
+        def prepare_w(c):
+            cols = slice(c * (N // 2), (c + 1) * (N // 2))
+            grouped = tile([P, N // 2, PACK], BF16, "w_grouped%d" % c)
+            nc.vector.tensor_copy(
+                grouped[:].rearrange("p (c i) j -> p c j i", i=4),
+                w_raw[c][:].rearrange("p j (c i) -> p c j i", i=4),
+            )
+            nc.vector.quantize_mx(
+                out=w_codes[:, cols].bitcast(FP8X4),
+                scales=w_plane[:, cols],
+                in_=grouped[:].rearrange("p m j -> p (m j)"),
+            )
+
+        HV = V // 2
+        z_codes = tile([P, V], U32, "z_codes")
+        z_plane = tile([P, V], U8, "z_plane")
+
+        def gather_half(hf):
+            ms = tile([P, PACK, HV], F32, "ms%d" % hf)
+            offsets = n1_t[:, hf * 16 : (hf + 1) * 16]
+            for pair in range(2):
+                lined = tile([P, 2, 2 * HV], F32, "lined%d%d" % (hf, pair))
+                for u in range(2):
+                    window = sq[2 * pair + u][:].indirect(offsets)
+                    if hf == 0:
+                        nc.vector.tensor_copy(lined[:, u, :], window)
+                    else:
+                        nc.scalar.activation(out=lined[:, u, :], in_=window, func=ACT.Copy)
+                both = lined[:].rearrange("p u (v e) -> p (u v) e", e=2)
+                nc.vector.scalar_tensor_tensor(
+                    out=ms[:, 2 * pair : 2 * pair + 2, :].rearrange("p u v -> p (u v)"),
+                    in0=both[:, :, 0],
+                    scalar=0.1,
+                    in1=both[:, :, 1],
+                    op0=ALU.add,
+                    op1=ALU.add,
+                )
+            return ms
+
+        def root_half(hf, ms):
+            root = tile([P, HV, PACK], F32, "root%d" % hf)
+            nc.scalar.activation(
+                out=root[:].rearrange("p (c i) t -> p c t i", i=4),
+                in_=ms[:].rearrange("p t (c i) -> p c t i", i=4),
+                func=ACT.Sqrt,
+            )
+            return root
+
+        def quantise_half(hf, root):
+            z = tile([P, HV, PACK], BF16, "z%d" % hf)
+            nc.vector.tensor_tensor(
+                out=z[:], in0=root[:], in1=gn_t[:].unsqueeze(1).to_broadcast([P, HV, PACK]), op=ALU.mult
+            )
+            cols = slice(hf * HV, (hf + 1) * HV)
+            nc.vector.quantize_mx(
+                out=z_codes[:, cols].bitcast(FP8X4),
+                scales=z_plane[:, cols],
+                in_=z[:].rearrange("p v t -> p (v t)"),
+            )
+
+        prepare_w(0)
+        ms0 = gather_half(0)
+        root0 = root_half(0, ms0)
+        prepare_w(1)
+        quantise_half(0, root0)
+        ms1 = gather_half(1)
+        root1 = root_half(1, ms1)
+        quantise_half(1, root1)
+
+        for mt in range(N // P):
+            bank = psum.tile([P, V], F32, name="h2_bank%d" % mt)
+            rows = slice(mt * P, (mt + 1) * P)
+            for hf in range(2):
+                cols = slice(hf * HV, (hf + 1) * HV)
+                nc.tensor.matmul_mx(
+                    out=bank[:, cols],
+                    lhsT=w_codes[:, rows].bitcast(FP8X4),
+                    lhsT_scale=w_plane[:, rows],
+                    rhs=z_codes[:, cols].bitcast(FP8X4),
+                    rhs_scale=z_plane[:, cols],
+                    start=True,
+                    stop=True,
+                )
+            h2 = tile([P, V], F32, "h2_%d" % mt)
+            if mt < 2:
+                nc.vector.tensor_copy(h2[:], bank[:])
+            else:
+                nc.scalar.copy(h2[:], bank[:])
+            gate = tile([P, V], F32, "gate%d" % mt)
+            picked = tile([P, V], F32, "picked%d" % mt)
+            for hf in range(2):
+                cols = slice(hf * HV, (hf + 1) * HV)
+                nc.scalar.activation(
+                    out=gate[:, cols], in_=h2[:].indirect(n2_t[:, hf * 8 : (hf + 1) * 8]), func=ACT.Sigmoid
+                )
+            for hf in range(2):
+                cols = slice(hf * HV, (hf + 1) * HV)
+                nc.vector.tensor_tensor(
+                    out=picked[:, cols],
+                    in0=h2[:].indirect(n3_t[:, hf * 8 : (hf + 1) * 8]),
+                    in1=gate[:, cols],
+                    op=ALU.mult,
+                )
+            rest = tile([P, V], F32, "rest%d" % mt)
+            nc.vector.scalar_tensor_tensor(
+                out=rest[:], in0=gate[:], scalar=1.0, in1=h2[:], op0=ALU.subtract, op1=ALU.mult
+            )
+            res = tile([P, V], F32, "res%d" % mt)
+            nc.vector.tensor_tensor(out=res[:], in0=picked[:], in1=rest[:], op=ALU.subtract)
+            nc.sync.dma_start(out[rows, :], res[:])

@@ -32,37 +32,37 @@ def tile_picked_hpqhprmstrack_none_p_kernel(
             nc.sync.dma_start(held[:], src)
             return held
 
-        def tile(shape, dtype, name):
-            return sb.tile(shape, dtype, name=name, align_bytes=64)
+        def tile(shape, dtype, name, tag=None):
+            return sb.tile(shape, dtype, name=name, tag=tag or name, align_bytes=64)
 
-        d_bytes_tab = tile([P, G], U8, "d_bytes_tab")
-        x_bytes_tab = tile([P, T], U8, "x_bytes_tab")
         plane = tile([P, H + S], U8, "plane")
-        nc.vector.memset(d_bytes_tab[:].bitcast(I32), 0)
-        nc.vector.memset(x_bytes_tab[:].bitcast(I32), 0)
         nc.vector.memset(plane[:].bitcast(I32), 0)
 
         k1_t = load_list(k1, "k1_t")
+        d_bytes_tab = tile([P, G], U8, "d_bytes_tab")
+        nc.sync.dma_start(
+            d_bytes_tab[:].bitcast(I32), d_scales[0].bitcast(I32).unsqueeze(1).to_broadcast([16, 8, G // 4])
+        )
         offs_t = load_list(offs, "offs_t")
+        x_bytes_tab = tile([P, T], U8, "x_bytes_tab")
+        nc.sync.dma_start(
+            x_bytes_tab[:].bitcast(I32), x_scales[0].bitcast(I32).unsqueeze(1).to_broadcast([16, 8, T // 4])
+        )
         d_tab = tile([P, G], U32, "d_tab")
         nc.sync.dma_start(d_tab[:].bitcast(I32), d_words[0].rearrange("p n t -> p (n t)").bitcast(I32))
-        nc.scalar.dma_start(d_bytes_tab[0:P:8, :].bitcast(I32), d_scales[0].bitcast(I32))
-        nc.scalar.dma_start(x_bytes_tab[0:P:8, :].bitcast(I32), x_scales[0].bitcast(I32))
         n1_t = load_list(n1, "n1_t")
         n2_t = load_list(n2, "n2_t")
-        n3_t = load_list(n3, "n3_t")
         x_tab = tile([P, T], U32, "x_tab")
         nc.sync.dma_start(x_tab[:].bitcast(I32), x_words[0].rearrange("p n t -> p (n t)").bitcast(I32))
+        n3_t = load_list(n3, "n3_t")
         gn_t = tile([P, PACK], F32, "gn_t")
-        nc.gpsimd.dma_start(gn_t[:], gn.rearrange("(p t) o -> p (t o)", t=PACK))
-        w_view = w1.rearrange("(p j) m -> p j m", j=PACK)
-        w_raw = []
-        for c in range(2):
-            raw = tile([P, PACK, N // 2], F32, "w_raw%d" % c)
-            nc.sync.dma_start(raw[:], w_view[:, :, c * (N // 2) : (c + 1) * (N // 2)])
-            w_raw.append(raw)
+        nc.sync.dma_start(gn_t[:], gn.rearrange("(p t) o -> p (t o)", t=PACK))
 
-        got_bytes = tile([P, H + S], U8, "got_bytes")
+        warm = tile([P, 2], F32, "warm")
+        nc.vector.memset(warm[:, 0:1], 1.0)
+        nc.scalar.activation(out=warm[:, 1:2], in_=warm[:, 0:1], func=ACT.Sqrt)
+
+        got_bytes = tile([P, H + S], U8, "got_bytes", "stage0")
         nc.vector.tensor_copy(got_bytes[:, 0:H], d_bytes_tab[:].indirect(k1_t[:]))
         nc.vector.tensor_copy(got_bytes[:, H : H + S], x_bytes_tab[:].indirect(offs_t[:]))
         dealt_bytes = tile([P, H + S], U8, "dealt_bytes")
@@ -72,145 +72,242 @@ def tile_picked_hpqhprmstrack_none_p_kernel(
         )
         nc.vector.tensor_copy(dealt_bytes[:, H : H + S].bitcast(I32), got_bytes[:, H : H + S].bitcast(I32))
         for j in range(4):
-            nc.scalar.dma_start(plane[j:P:32, :].bitcast(I32), dealt_bytes[8 * j : P : 32, :].bitcast(I32))
+            nc.sync.dma_start(plane[j:P:32, :].bitcast(I32), dealt_bytes[8 * j : P : 32, :].bitcast(I32))
 
-        d_got = tile([P, H], U32, "d_got")
+        d_got = tile([P, H], U32, "d_got", "stage2")
         nc.vector.tensor_copy(d_got[:], d_tab[:].indirect(k1_t[:]))
         d_dealt = tile([P, H], U32, "d_dealt")
         nc.vector.tensor_copy(
             d_dealt[:].rearrange("p (t c i) -> p c t i", t=PACK, i=4),
             d_got[:].rearrange("p (c i t) -> p c t i", t=PACK, i=4),
         )
-        x_got = tile([P, S], U32, "x_got")
-        nc.vector.tensor_copy(x_got[:], x_tab[:].indirect(offs_t[:]))
+        w_view = w1.rearrange("(p j) m -> p j m", j=PACK)
+        w_raw = []
+        for c in range(2):
+            raw = tile([P, PACK, N // 2], F32, "w_raw%d" % c, "stage%d" % (2 * c))
+            nc.sync.dma_start(raw[:], w_view[:, :, c * (N // 2) : (c + 1) * (N // 2)])
+            w_raw.append(raw)
 
-        sq = []
-        for t in range(PACK):
-            bank = psum.tile([P, S], F32, name="h_bank%d" % t)
-            cols = slice(t * P, (t + 1) * P)
-            nc.tensor.matmul_mx(
-                out=bank[:],
-                lhsT=d_dealt[:, cols].bitcast(FP8X4),
-                lhsT_scale=plane[:, cols],
-                rhs=x_got[:].bitcast(FP8X4),
-                rhs_scale=plane[:, H : H + S],
-                start=True,
-                stop=True,
-            )
-            sq_t = tile([P, S], F32, "sq%d" % t)
-            nc.scalar.activation(out=sq_t[:], in_=bank[:], func=ACT.Square, scale=0.0625)
-            sq.append(sq_t)
+        x_got = [tile([P, S // 2], U32, "x_got%d" % hs) for hs in range(2)]
+        for hs in range(2):
+            nc.vector.tensor_copy(x_got[hs][:], x_tab[:].indirect(offs_t[:, hs * 16 : (hs + 1) * 16]))
 
-        w_codes = tile([P, N], U32, "w_codes")
-        w_plane = tile([P, N], U8, "w_plane")
+        sq = [tile([P, S], F32, "sq%d" % t) for t in range(PACK)]
+        for pair in range(2):
+            for hs in range(2):
+                for t in (2 * pair, 2 * pair + 1):
+                    bank = psum.tile([P, S // 2], F32, name="h_bank%d%d" % (t, hs), tag="bank%d" % (2 * t + hs))
+                    cols = slice(t * P, (t + 1) * P)
+                    nc.tensor.matmul_mx(
+                        out=bank[:],
+                        lhsT=d_dealt[:, cols].bitcast(FP8X4),
+                        lhsT_scale=plane[:, cols],
+                        rhs=x_got[hs][:].bitcast(FP8X4),
+                        rhs_scale=plane[:, H + hs * (S // 2) : H + (hs + 1) * (S // 2)],
+                        start=True,
+                        stop=True,
+                    )
+                    nc.scalar.activation(
+                        out=sq[t][:, hs * (S // 2) : (hs + 1) * (S // 2)], in_=bank[:], func=ACT.Square, scale=0.0625
+                    )
 
-        def prepare_w(c):
-            cols = slice(c * (N // 2), (c + 1) * (N // 2))
-            grouped = tile([P, N // 2, PACK], BF16, "w_grouped%d" % c)
-            nc.vector.tensor_copy(
-                grouped[:].rearrange("p (c i) j -> p c j i", i=4),
+        w_grouped = [tile([P, N // 2, PACK], BF16, "w_grouped%d" % c) for c in range(2)]
+        w_codes = [tile([P, N // 2], U32, "w_codes%d" % c) for c in range(2)]
+        w_plane = [tile([P, N // 2], U8, "w_plane%d" % c) for c in range(2)]
+
+        def group_w(eng, c):
+            eng.tensor_copy(
+                w_grouped[c][:].rearrange("p (c i) j -> p c j i", i=4),
                 w_raw[c][:].rearrange("p j (c i) -> p c j i", i=4),
             )
+
+        def quantise_w(c):
             nc.vector.quantize_mx(
-                out=w_codes[:, cols].bitcast(FP8X4),
-                scales=w_plane[:, cols],
-                in_=grouped[:].rearrange("p m j -> p (m j)"),
+                out=w_codes[c][:].bitcast(FP8X4),
+                scales=w_plane[c][:],
+                in_=w_grouped[c][:].rearrange("p m j -> p (m j)"),
             )
 
         HV = V // 2
-        z_codes = tile([P, V], U32, "z_codes")
-        z_plane = tile([P, V], U8, "z_plane")
+        QV = V // 4
+        parts = {"A": (0, HV), "B": (HV, HV), "B1": (HV, QV), "B2": (HV + QV, QV)}
+        lined = {
+            (a, pair): tile([P, 2, 2 * parts[a][1]], F32, "lined%s%d" % (a, pair))
+            for a, pair in (("A", 0), ("A", 1), ("B", 0), ("B1", 1), ("B2", 1))
+        }
+        ms = [tile([P, PACK, HV], F32, "ms%d" % hf) for hf in range(2)]
+        root = {a: tile([P, parts[a][1], PACK], F32, "root" + a) for a in ("A", "B1", "B2")}
+        z = [tile([P, HV, PACK], BF16, "z%d" % hf) for hf in range(2)]
+        z_codes = [tile([P, HV], U32, "z_codes%d" % hf) for hf in range(2)]
+        z_plane = [tile([P, HV], U8, "z_plane%d" % hf) for hf in range(2)]
 
-        def gather_half(hf):
-            ms = tile([P, PACK, HV], F32, "ms%d" % hf)
-            offsets = n1_t[:, hf * 16 : (hf + 1) * 16]
-            for pair in range(2):
-                lined = tile([P, 2, 2 * HV], F32, "lined%d%d" % (hf, pair))
-                for u in range(2):
-                    window = sq[2 * pair + u][:].indirect(offsets)
-                    if hf == 0:
-                        nc.vector.tensor_copy(lined[:, u, :], window)
-                    else:
-                        nc.scalar.activation(out=lined[:, u, :], in_=window, func=ACT.Copy)
-                both = lined[:].rearrange("p u (v e) -> p (u v) e", e=2)
-                nc.vector.scalar_tensor_tensor(
-                    out=ms[:, 2 * pair : 2 * pair + 2, :].rearrange("p u v -> p (u v)"),
-                    in0=both[:, :, 0],
-                    scalar=0.1,
-                    in1=both[:, :, 1],
-                    op0=ALU.add,
-                    op1=ALU.add,
-                )
-            return ms
+        def line_up(eng, t, a):
+            v0, nv = parts[a]
+            window = sq[t][:].indirect(n1_t[:, v0 // 8 : (v0 + nv) // 8])
+            if eng == "V":
+                nc.vector.tensor_copy(lined[a, t // 2][:, t % 2, :], window)
+            else:
+                nc.scalar.activation(out=lined[a, t // 2][:, t % 2, :], in_=window, func=ACT.Copy)
 
-        def root_half(hf, ms):
-            root = tile([P, HV, PACK], F32, "root%d" % hf)
+        def add_pairs(eng, a, pair):
+            v0, nv = parts[a]
+            both = lined[a, pair][:].rearrange("p u (v e) -> p u v e", e=2)
+            eng.tensor_tensor(
+                out=ms[v0 // HV][:, 2 * pair : 2 * pair + 2, v0 % HV : v0 % HV + nv],
+                in0=both[:, :, :, 0],
+                in1=both[:, :, :, 1],
+                op=ALU.add,
+            )
+
+        def take_root(a):
+            v0, nv = parts[a]
             nc.scalar.activation(
-                out=root[:].rearrange("p (c i) t -> p c t i", i=4),
-                in_=ms[:].rearrange("p t (c i) -> p c t i", i=4),
+                out=root[a][:].rearrange("p (c i) t -> p c t i", i=4),
+                in_=ms[v0 // HV][:, :, v0 % HV : v0 % HV + nv].rearrange("p t (c i) -> p c t i", i=4),
                 func=ACT.Sqrt,
+                bias=0.1,
             )
-            return root
 
-        def quantise_half(hf, root):
-            z = tile([P, HV, PACK], BF16, "z%d" % hf)
+        def gain(a):
+            v0, nv = parts[a]
             nc.vector.tensor_tensor(
-                out=z[:], in0=root[:], in1=gn_t[:].unsqueeze(1).to_broadcast([P, HV, PACK]), op=ALU.mult
+                out=z[v0 // HV][:, v0 % HV : v0 % HV + nv, :],
+                in0=root[a][:],
+                in1=gn_t[:].unsqueeze(1).to_broadcast([P, nv, PACK]),
+                op=ALU.mult,
             )
-            cols = slice(hf * HV, (hf + 1) * HV)
+
+        def quantise_z(hf):
             nc.vector.quantize_mx(
-                out=z_codes[:, cols].bitcast(FP8X4),
-                scales=z_plane[:, cols],
-                in_=z[:].rearrange("p v t -> p (v t)"),
+                out=z_codes[hf][:].bitcast(FP8X4),
+                scales=z_plane[hf][:],
+                in_=z[hf][:].rearrange("p v t -> p (v t)"),
             )
 
-        prepare_w(0)
-        ms0 = gather_half(0)
-        root0 = root_half(0, ms0)
-        prepare_w(1)
-        quantise_half(0, root0)
-        ms1 = gather_half(1)
-        root1 = root_half(1, ms1)
-        quantise_half(1, root1)
+        MT = N // P
+        h2 = [tile([P, V], F32, "h2_%d" % mt) for mt in range(MT)]
+        bank_a = psum.tile([P, MT, HV], F32, name="h2_bank_a", tag="bank0")
+        bank_b = [psum.tile([P, HV], F32, name="h2_bank_b%d" % mt, tag="bank%d" % (mt + 1)) for mt in range(MT)]
 
-        for mt in range(N // P):
-            bank = psum.tile([P, V], F32, name="h2_bank%d" % mt)
-            rows = slice(mt * P, (mt + 1) * P)
-            for hf in range(2):
-                cols = slice(hf * HV, (hf + 1) * HV)
+        def second_product(hf):
+            for mt in range(MT):
+                cols = slice((mt % 2) * P, (mt % 2 + 1) * P)
                 nc.tensor.matmul_mx(
-                    out=bank[:, cols],
-                    lhsT=w_codes[:, rows].bitcast(FP8X4),
-                    lhsT_scale=w_plane[:, rows],
-                    rhs=z_codes[:, cols].bitcast(FP8X4),
-                    rhs_scale=z_plane[:, cols],
+                    out=bank_a[:, mt, :] if hf == 0 else bank_b[mt][:],
+                    lhsT=w_codes[mt // 2][:, cols].bitcast(FP8X4),
+                    lhsT_scale=w_plane[mt // 2][:, cols],
+                    rhs=z_codes[hf][:].bitcast(FP8X4),
+                    rhs_scale=z_plane[hf][:],
                     start=True,
                     stop=True,
                 )
-            h2 = tile([P, V], F32, "h2_%d" % mt)
-            if mt < 2:
-                nc.vector.tensor_copy(h2[:], bank[:])
-            else:
-                nc.scalar.copy(h2[:], bank[:])
-            gate = tile([P, V], F32, "gate%d" % mt)
-            picked = tile([P, V], F32, "picked%d" % mt)
+
+        group_w(nc.vector, 0)
+        quantise_w(0)
+        line_up("V", 0, "A")
+        line_up("V", 1, "A")
+        line_up("V", 2, "A")
+        line_up("S", 3, "A")
+        add_pairs(nc.vector, "A", 0)
+        line_up("S", 1, "B")
+        line_up("V", 0, "B")
+        add_pairs(nc.vector, "A", 1)
+        line_up("S", 2, "B1")
+        group_w(nc.vector, 1)
+        take_root("A")
+        add_pairs(nc.vector, "B", 0)
+        line_up("S", 3, "B1")
+        quantise_w(1)
+        line_up("S", 2, "B2")
+        line_up("S", 3, "B2")
+        gain("A")
+        add_pairs(nc.vector, "B1", 1)
+        take_root("B1")
+        quantise_z(0)
+        second_product(0)
+        add_pairs(nc.vector, "B2", 1)
+        take_root("B2")
+        gain("B1")
+        gain("B2")
+        quantise_z(1)
+        second_product(1)
+
+        gate = [tile([P, V], F32, "gate%d" % mt) for mt in range(MT)]
+        picked = [tile([P, V], F32, "picked%d" % mt) for mt in range(MT)]
+        part = [tile([P, V], F32, "part%d" % mt) for mt in range(MT)]
+        moved = [tile([P, V], F32, "moved%d" % mt) for mt in (0, 1)]
+        res = [tile([P, V], F32, "res%d" % mt) for mt in range(MT)]
+
+        def half(hf):
+            return slice(hf * HV, (hf + 1) * HV), slice(hf * 8, (hf + 1) * 8)
+
+        def gates(mt):
             for hf in range(2):
-                cols = slice(hf * HV, (hf + 1) * HV)
-                nc.scalar.activation(
-                    out=gate[:, cols], in_=h2[:].indirect(n2_t[:, hf * 8 : (hf + 1) * 8]), func=ACT.Sigmoid
-                )
+                cols, entries = half(hf)
+                nc.scalar.activation(out=gate[mt][:, cols], in_=h2[mt][:].indirect(n2_t[:, entries]), func=ACT.Sigmoid)
+
+        def pick(mt):
             for hf in range(2):
-                cols = slice(hf * HV, (hf + 1) * HV)
-                nc.vector.tensor_tensor(
-                    out=picked[:, cols],
-                    in0=h2[:].indirect(n3_t[:, hf * 8 : (hf + 1) * 8]),
-                    in1=gate[:, cols],
-                    op=ALU.mult,
-                )
-            rest = tile([P, V], F32, "rest%d" % mt)
-            nc.vector.scalar_tensor_tensor(
-                out=rest[:], in0=gate[:], scalar=1.0, in1=h2[:], op0=ALU.subtract, op1=ALU.mult
+                cols, entries = half(hf)
+                nc.scalar.activation(out=picked[mt][:, cols], in_=h2[mt][:].indirect(n3_t[:, entries]), func=ACT.Copy)
+
+        def pick_times_gate(mt, hf):
+            cols, entries = half(hf)
+            nc.vector.tensor_tensor(
+                out=picked[mt][:, cols], in0=h2[mt][:].indirect(n3_t[:, entries]), in1=gate[mt][:, cols], op=ALU.mult
             )
-            res = tile([P, V], F32, "res%d" % mt)
-            nc.vector.tensor_tensor(out=res[:], in0=picked[:], in1=rest[:], op=ALU.subtract)
-            nc.sync.dma_start(out[rows, :], res[:])
+
+        def take_rest(mt):
+            nc.vector.scalar_tensor_tensor(
+                out=part[mt][:], in0=gate[mt][:], scalar=1.0, in1=h2[mt][:], op0=ALU.subtract, op1=ALU.mult
+            )
+
+        def store(mt):
+            nc.sync.dma_start(out[mt * P : (mt + 1) * P, :], res[mt][:])
+
+        def finish(mt):
+            nc.vector.tensor_tensor(out=res[mt][:], in0=picked[mt][:], in1=part[mt][:], op=ALU.subtract)
+            store(mt)
+
+        def take_diff(mt):
+            nc.vector.tensor_tensor(out=part[mt][:], in0=picked[mt][:], in1=h2[mt][:], op=ALU.subtract)
+
+        def weigh(mt, cols):
+            nc.vector.tensor_tensor(
+                out=moved[mt - 2][:, cols], in0=part[mt][:, cols], in1=gate[mt][:, cols], op=ALU.mult
+            )
+
+        def add_back(mt, cols):
+            nc.vector.tensor_tensor(out=res[mt][:, cols], in0=moved[mt - 2][:, cols], in1=h2[mt][:, cols], op=ALU.add)
+
+        warm2 = tile([P, 1], F32, "warm2")
+        nc.scalar.activation(out=warm2[:], in_=root["B2"][:, 0, 0:1], func=ACT.Sigmoid)
+        for mt in range(MT):
+            nc.vector.tensor_copy(h2[mt][:, 0:HV], bank_a[:, mt, :])
+        nc.scalar.copy(h2[0][:, HV:V], bank_b[0][:])
+        for mt in range(1, MT):
+            nc.vector.tensor_copy(h2[mt][:, HV:V], bank_b[mt][:])
+        gates(0)
+        gates(1)
+        pick(2)
+        gates(2)
+        pick(3)
+        gates(3)
+        pick_times_gate(0, 0)
+        pick_times_gate(0, 1)
+        take_rest(0)
+        pick_times_gate(1, 0)
+        finish(0)
+        pick_times_gate(1, 1)
+        take_rest(1)
+        take_diff(2)
+        finish(1)
+        weigh(2, slice(0, V))
+        take_diff(3)
+        add_back(2, slice(0, V))
+        store(2)
+        for hf in range(2):
+            weigh(3, half(hf)[0])
+        for hf in range(2):
+            add_back(3, half(hf)[0])
+        store(3)

@@ -35,19 +35,18 @@ def tile_picked_hpqhprmstrack_none_p_kernel(
         def tile(shape, dtype, name, tag=None):
             return sb.tile(shape, dtype, name=name, tag=tag or name, align_bytes=64)
 
+        x_bytes_tab = tile([P, T], U8, "x_bytes_tab")
+        nc.vector.memset(x_bytes_tab[:].bitcast(I32), 0)
         plane = tile([P, H + S], U8, "plane")
         nc.vector.memset(plane[:].bitcast(I32), 0)
 
-        k1_t = load_list(k1, "k1_t")
         d_bytes_tab = tile([P, G], U8, "d_bytes_tab")
         nc.sync.dma_start(
             d_bytes_tab[:].bitcast(I32), d_scales[0].bitcast(I32).unsqueeze(1).to_broadcast([16, 8, G // 4])
         )
+        k1_t = load_list(k1, "k1_t")
         offs_t = load_list(offs, "offs_t")
-        x_bytes_tab = tile([P, T], U8, "x_bytes_tab")
-        nc.sync.dma_start(
-            x_bytes_tab[:].bitcast(I32), x_scales[0].bitcast(I32).unsqueeze(1).to_broadcast([16, 8, T // 4])
-        )
+        nc.sync.dma_start(x_bytes_tab[0:P:8, :].bitcast(I32), x_scales[0].bitcast(I32))
         d_tab = tile([P, G], U32, "d_tab")
         nc.sync.dma_start(d_tab[:].bitcast(I32), d_words[0].rearrange("p n t -> p (n t)").bitcast(I32))
         n1_t = load_list(n1, "n1_t")
@@ -74,13 +73,15 @@ def tile_picked_hpqhprmstrack_none_p_kernel(
         for j in range(4):
             nc.sync.dma_start(plane[j:P:32, :].bitcast(I32), dealt_bytes[8 * j : P : 32, :].bitcast(I32))
 
-        d_got = tile([P, H], U32, "d_got", "stage2")
-        nc.vector.tensor_copy(d_got[:], d_tab[:].indirect(k1_t[:]))
+        d_got = [tile([P, H // 2], U32, "d_got%d" % hd, ("d_got0", "stage2")[hd]) for hd in range(2)]
+        for hd in range(2):
+            nc.vector.tensor_copy(d_got[hd][:], d_tab[:].indirect(k1_t[:, hd * 16 : (hd + 1) * 16]))
         d_dealt = tile([P, H], U32, "d_dealt")
-        nc.vector.tensor_copy(
-            d_dealt[:].rearrange("p (t c i) -> p c t i", t=PACK, i=4),
-            d_got[:].rearrange("p (c i t) -> p c t i", t=PACK, i=4),
-        )
+        for hd in range(2):
+            nc.vector.tensor_copy(
+                d_dealt[:].rearrange("p (t h c i) -> p h c t i", t=PACK, h=2, i=4)[:, hd],
+                d_got[hd][:].rearrange("p (c i t) -> p c t i", t=PACK, i=4),
+            )
         w_view = w1.rearrange("(p j) m -> p j m", j=PACK)
         w_raw = []
         for c in range(2):
@@ -309,5 +310,6 @@ def tile_picked_hpqhprmstrack_none_p_kernel(
         for hf in range(2):
             weigh(3, half(hf)[0])
         for hf in range(2):
-            add_back(3, half(hf)[0])
-        store(3)
+            cols = half(hf)[0]
+            add_back(3, cols)
+            nc.sync.dma_start(out[3 * P : 4 * P, cols], res[3][:, cols])

@@ -35,20 +35,22 @@ def tile_picked_hpqhprmstrack_none_p_kernel(
         def tile(shape, dtype, name, tag=None):
             return sb.tile(shape, dtype, name=name, tag=tag or name, align_bytes=64)
 
+        d_bytes_tab = tile([P, G], U8, "d_bytes_tab")
+        nc.vector.memset(d_bytes_tab[:].bitcast(I32), 0)
         x_bytes_tab = tile([P, T], U8, "x_bytes_tab")
         nc.vector.memset(x_bytes_tab[:].bitcast(I32), 0)
         plane = tile([P, H + S], U8, "plane")
         nc.vector.memset(plane[:].bitcast(I32), 0)
 
-        d_bytes_tab = tile([P, G], U8, "d_bytes_tab")
-        nc.sync.dma_start(
-            d_bytes_tab[:].bitcast(I32), d_scales[0].bitcast(I32).unsqueeze(1).to_broadcast([16, 8, G // 4])
-        )
+        d_tab = tile([P, G], U32, "d_tab")
+        d_rows = d_words[0].rearrange("p n t -> p (n t)").bitcast(I32)
+        head = G // 4
+        nc.sync.dma_start(d_tab[:, 0:head].bitcast(I32), d_rows[:, 0:head])
         k1_t = load_list(k1, "k1_t")
+        nc.sync.dma_start(d_bytes_tab[0:P:8, :].bitcast(I32), d_scales[0].bitcast(I32))
         offs_t = load_list(offs, "offs_t")
         nc.sync.dma_start(x_bytes_tab[0:P:8, :].bitcast(I32), x_scales[0].bitcast(I32))
-        d_tab = tile([P, G], U32, "d_tab")
-        nc.sync.dma_start(d_tab[:].bitcast(I32), d_words[0].rearrange("p n t -> p (n t)").bitcast(I32))
+        nc.sync.dma_start(d_tab[:, head:G].bitcast(I32), d_rows[:, head:G])
         n1_t = load_list(n1, "n1_t")
         n2_t = load_list(n2, "n2_t")
         x_tab = tile([P, T], U32, "x_tab")

from contextlib import ExitStack

import concourse.mybir as mybir

F32 = mybir.dt.float32
BF16 = mybir.dt.bfloat16
I32 = mybir.dt.int32
U32 = mybir.dt.uint32
U16 = mybir.dt.uint16
U8 = mybir.dt.uint8
FP8X4 = mybir.dt.float8_e4m3fn_x4
ACT = mybir.ActivationFunctionType
ALU = mybir.AluOpType

P = 128
PACK = 4
K, T, S, V, N, G, H = 512, 2048, 512, 256, 512, 2048, 512
FLOPS = 2 * K * H * S + 2 * H * N * V


def tile_picked_hpqhprmstrack_none_p_kernel(
    tc, x_words, x_scales, d_words, d_scales, gn, w1, offs, k1, n1, n2, n3, out
):
    nc = tc.nc
    with ExitStack() as ctx:
        lists = ctx.enter_context(tc.tile_pool(name="lists", bufs=1))
        sb = ctx.enter_context(tc.tile_pool(name="sb", bufs=1))
        psum = ctx.enter_context(tc.psum_pool(name="psum", bufs=1))

        def load_list(src, name):
            held = lists.tile(list(src.shape), U16, name=name)
            nc.sync.dma_start(held[:], src)
            return held

        def tile(shape, dtype, name, tag=None):
            return sb.tile(shape, dtype, name=name, tag=tag or name, align_bytes=64)

        d_bytes_tab = tile([P, G], U8, "d_bytes_tab")
        nc.vector.memset(d_bytes_tab[:].bitcast(I32), 0)
        x_bytes_tab = tile([P, T], U8, "x_bytes_tab")
        nc.vector.memset(x_bytes_tab[:].bitcast(I32), 0)
        plane = tile([P, H + S], U8, "plane")
        nc.vector.memset(plane[:].bitcast(I32), 0)

        d_tab = tile([P, G], U32, "d_tab")
        d_rows = d_words[0].rearrange("p n t -> p (n t)").bitcast(I32)
        head = G // 4
        nc.sync.dma_start(d_tab[:, 0:head].bitcast(I32), d_rows[:, 0:head])
        k1_t = load_list(k1, "k1_t")
        nc.sync.dma_start(d_bytes_tab[0:P:8, :].bitcast(I32), d_scales[0].bitcast(I32))
        offs_t = load_list(offs, "offs_t")
        nc.sync.dma_start(x_bytes_tab[0:P:8, :].bitcast(I32), x_scales[0].bitcast(I32))
        nc.sync.dma_start(d_tab[:, head:G].bitcast(I32), d_rows[:, head:G])
        n1_t = load_list(n1, "n1_t")
        n2_t = load_list(n2, "n2_t")
        x_tab = tile([P, T], U32, "x_tab")
        nc.sync.dma_start(x_tab[:].bitcast(I32), x_words[0].rearrange("p n t -> p (n t)").bitcast(I32))
        n3_t = load_list(n3, "n3_t")
        gn_t = tile([P, PACK], F32, "gn_t")
        nc.sync.dma_start(gn_t[:], gn.rearrange("(p t) o -> p (t o)", t=PACK))

        warm = tile([P, 2], F32, "warm")
        nc.vector.memset(warm[:, 0:1], 1.0)
        nc.scalar.activation(out=warm[:, 1:2], in_=warm[:, 0:1], func=ACT.Sqrt)

        got_bytes = tile([P, H + S], U8, "got_bytes", "stage0")
        nc.vector.tensor_copy(got_bytes[:, 0:H], d_bytes_tab[:].indirect(k1_t[:]))
        nc.vector.tensor_copy(got_bytes[:, H : H + S], x_bytes_tab[:].indirect(offs_t[:]))
        dealt_bytes = tile([P, H + S], U8, "dealt_bytes")
        nc.vector.tensor_copy(
            dealt_bytes[:, 0:H].rearrange("p (t m) -> p t m", t=PACK),
            got_bytes[:, 0:H].rearrange("p (m t) -> p t m", t=PACK),
        )
        nc.vector.tensor_copy(dealt_bytes[:, H : H + S].bitcast(I32), got_bytes[:, H : H + S].bitcast(I32))
        for j in range(4):
            nc.sync.dma_start(plane[j:P:32, :].bitcast(I32), dealt_bytes[8 * j : P : 32, :].bitcast(I32))

        d_got = [tile([P, H // 2], U32, "d_got%d" % hd, ("d_got0", "stage2")[hd]) for hd in range(2)]
        for hd in range(2):
            nc.vector.tensor_copy(d_got[hd][:], d_tab[:].indirect(k1_t[:, hd * 16 : (hd + 1) * 16]))
        d_dealt = tile([P, H], U32, "d_dealt")
        for hd in range(2):
            nc.vector.tensor_copy(
                d_dealt[:].rearrange("p (t h c i) -> p h c t i", t=PACK, h=2, i=4)[:, hd],
                d_got[hd][:].rearrange("p (c i t) -> p c t i", t=PACK, i=4),
            )
        w_view = w1.rearrange("(p j) m -> p j m", j=PACK)
        w_raw = []
        for c in range(2):
            raw = tile([P, PACK, N // 2], F32, "w_raw%d" % c, "stage%d" % (2 * c))
            nc.sync.dma_start(raw[:], w_view[:, :, c * (N // 2) : (c + 1) * (N // 2)])
            w_raw.append(raw)

        x_got = [tile([P, S // 2], U32, "x_got%d" % hs) for hs in range(2)]
        for hs in range(2):
            nc.vector.tensor_copy(x_got[hs][:], x_tab[:].indirect(offs_t[:, hs * 16 : (hs + 1) * 16]))

        sq = [tile([P, S], F32, "sq%d" % t) for t in range(PACK)]
        for pair in range(2):
            for hs in range(2):
                for t in (2 * pair, 2 * pair + 1):
                    bank = psum.tile([P, S // 2], F32, name="h_bank%d%d" % (t, hs), tag="bank%d" % (2 * t + hs))
                    cols = slice(t * P, (t + 1) * P)
                    nc.tensor.matmul_mx(
                        out=bank[:],
                        lhsT=d_dealt[:, cols].bitcast(FP8X4),
                        lhsT_scale=plane[:, cols],
                        rhs=x_got[hs][:].bitcast(FP8X4),
                        rhs_scale=plane[:, H + hs * (S // 2) : H + (hs + 1) * (S // 2)],
                        start=True,
                        stop=True,
                    )
                    nc.scalar.activation(
                        out=sq[t][:, hs * (S // 2) : (hs + 1) * (S // 2)], in_=bank[:], func=ACT.Square, scale=0.0625
                    )

        w_grouped = [tile([P, N // 2, PACK], BF16, "w_grouped%d" % c) for c in range(2)]
        w_codes = [tile([P, N // 2], U32, "w_codes%d" % c) for c in range(2)]
        w_plane = [tile([P, N // 2], U8, "w_plane%d" % c) for c in range(2)]

        def group_w(eng, c):
            eng.tensor_copy(
                w_grouped[c][:].rearrange("p (c i) j -> p c j i", i=4),
                w_raw[c][:].rearrange("p j (c i) -> p c j i", i=4),
            )

        def quantise_w(c):
            nc.vector.quantize_mx(
                out=w_codes[c][:].bitcast(FP8X4),
                scales=w_plane[c][:],
                in_=w_grouped[c][:].rearrange("p m j -> p (m j)"),
            )

        HV = V // 2
        QV = V // 4
        parts = {"A": (0, HV), "B": (HV, HV), "B1": (HV, QV), "B2": (HV + QV, QV)}
        lined = {
            (a, pair): tile([P, 2, 2 * parts[a][1]], F32, "lined%s%d" % (a, pair))
            for a, pair in (("A", 0), ("A", 1), ("B", 0), ("B1", 1), ("B2", 1))
        }
        ms = [tile([P, PACK, HV], F32, "ms%d" % hf) for hf in range(2)]
        root = {a: tile([P, parts[a][1], PACK], F32, "root" + a) for a in ("A", "B1", "B2")}
        z = [tile([P, HV, PACK], BF16, "z%d" % hf) for hf in range(2)]
        z_codes = [tile([P, HV], U32, "z_codes%d" % hf) for hf in range(2)]
        z_plane = [tile([P, HV], U8, "z_plane%d" % hf) for hf in range(2)]

        def line_up(eng, t, a):
            v0, nv = parts[a]
            window = sq[t][:].indirect(n1_t[:, v0 // 8 : (v0 + nv) // 8])
            if eng == "V":
                nc.vector.tensor_copy(lined[a, t // 2][:, t % 2, :], window)
            else:
                nc.scalar.activation(out=lined[a, t // 2][:, t % 2, :], in_=window, func=ACT.Copy)

        def add_pairs(eng, a, pair):
            v0, nv = parts[a]
            both = lined[a, pair][:].rearrange("p u (v e) -> p u v e", e=2)
            eng.tensor_tensor(
                out=ms[v0 // HV][:, 2 * pair : 2 * pair + 2, v0 % HV : v0 % HV + nv],
                in0=both[:, :, :, 0],
                in1=both[:, :, :, 1],
                op=ALU.add,
            )

        def take_root(a):
            v0, nv = parts[a]
            nc.scalar.activation(
                out=root[a][:].rearrange("p (c i) t -> p c t i", i=4),
                in_=ms[v0 // HV][:, :, v0 % HV : v0 % HV + nv].rearrange("p t (c i) -> p c t i", i=4),
                func=ACT.Sqrt,
                bias=0.1,
            )

        def gain(a):
            v0, nv = parts[a]
            nc.vector.tensor_tensor(
                out=z[v0 // HV][:, v0 % HV : v0 % HV + nv, :],
                in0=root[a][:],
                in1=gn_t[:].unsqueeze(1).to_broadcast([P, nv, PACK]),
                op=ALU.mult,
            )

        def quantise_z(hf):
            nc.vector.quantize_mx(
                out=z_codes[hf][:].bitcast(FP8X4),
                scales=z_plane[hf][:],
                in_=z[hf][:].rearrange("p v t -> p (v t)"),
            )

        MT = N // P
        h2 = [tile([P, V], F32, "h2_%d" % mt) for mt in range(MT)]
        bank_a = psum.tile([P, MT, HV], F32, name="h2_bank_a", tag="bank0")
        bank_b = [psum.tile([P, HV], F32, name="h2_bank_b%d" % mt, tag="bank%d" % (mt + 1)) for mt in range(MT)]

        def second_product(hf):
            for mt in range(MT):
                cols = slice((mt % 2) * P, (mt % 2 + 1) * P)
                nc.tensor.matmul_mx(
                    out=bank_a[:, mt, :] if hf == 0 else bank_b[mt][:],
                    lhsT=w_codes[mt // 2][:, cols].bitcast(FP8X4),
                    lhsT_scale=w_plane[mt // 2][:, cols],
                    rhs=z_codes[hf][:].bitcast(FP8X4),
                    rhs_scale=z_plane[hf][:],
                    start=True,
                    stop=True,
                )

        group_w(nc.vector, 0)
        quantise_w(0)
        line_up("V", 0, "A")
        line_up("V", 1, "A")
        line_up("V", 2, "A")
        line_up("S", 3, "A")
        add_pairs(nc.vector, "A", 0)
        line_up("S", 1, "B")
        line_up("V", 0, "B")
        add_pairs(nc.vector, "A", 1)
        line_up("S", 2, "B1")
        group_w(nc.vector, 1)
        take_root("A")
        add_pairs(nc.vector, "B", 0)
        line_up("S", 3, "B1")
        quantise_w(1)
        line_up("S", 2, "B2")
        line_up("S", 3, "B2")
        gain("A")
        add_pairs(nc.vector, "B1", 1)
        take_root("B1")
        quantise_z(0)
        second_product(0)
        add_pairs(nc.vector, "B2", 1)
        take_root("B2")
        gain("B1")
        gain("B2")
        quantise_z(1)
        second_product(1)

        gate = [tile([P, V], F32, "gate%d" % mt) for mt in range(MT)]
        picked = [tile([P, V], F32, "picked%d" % mt) for mt in range(MT)]
        part = [tile([P, V], F32, "part%d" % mt) for mt in range(MT)]
        moved = [tile([P, V], F32, "moved%d" % mt) for mt in (0, 1)]
        res = [tile([P, V], F32, "res%d" % mt) for mt in range(MT)]

        def half(hf):
            return slice(hf * HV, (hf + 1) * HV), slice(hf * 8, (hf + 1) * 8)

        def gates(mt):
            for hf in range(2):
                cols, entries = half(hf)
                nc.scalar.activation(out=gate[mt][:, cols], in_=h2[mt][:].indirect(n2_t[:, entries]), func=ACT.Sigmoid)

        def pick(mt):
            for hf in range(2):
                cols, entries = half(hf)
                nc.scalar.activation(out=picked[mt][:, cols], in_=h2[mt][:].indirect(n3_t[:, entries]), func=ACT.Copy)

        def pick_times_gate(mt, hf):
            cols, entries = half(hf)
            nc.vector.tensor_tensor(
                out=picked[mt][:, cols], in0=h2[mt][:].indirect(n3_t[:, entries]), in1=gate[mt][:, cols], op=ALU.mult
            )

        def take_rest(mt):
            nc.vector.scalar_tensor_tensor(
                out=part[mt][:], in0=gate[mt][:], scalar=1.0, in1=h2[mt][:], op0=ALU.subtract, op1=ALU.mult
            )

        def store(mt):
            nc.sync.dma_start(out[mt * P : (mt + 1) * P, :], res[mt][:])

        def finish(mt):
            nc.vector.tensor_tensor(out=res[mt][:], in0=picked[mt][:], in1=part[mt][:], op=ALU.subtract)
            store(mt)

        def take_diff(mt):
            nc.vector.tensor_tensor(out=part[mt][:], in0=picked[mt][:], in1=h2[mt][:], op=ALU.subtract)

        def weigh(mt, cols):
            nc.vector.tensor_tensor(
                out=moved[mt - 2][:, cols], in0=part[mt][:, cols], in1=gate[mt][:, cols], op=ALU.mult
            )

        def add_back(mt, cols):
            nc.vector.tensor_tensor(out=res[mt][:, cols], in0=moved[mt - 2][:, cols], in1=h2[mt][:, cols], op=ALU.add)

        warm2 = tile([P, 1], F32, "warm2")
        nc.scalar.activation(out=warm2[:], in_=root["B2"][:, 0, 0:1], func=ACT.Sigmoid)
        for mt in range(MT):
            nc.vector.tensor_copy(h2[mt][:, 0:HV], bank_a[:, mt, :])
        nc.scalar.copy(h2[0][:, HV:V], bank_b[0][:])
        for mt in range(1, MT):
            nc.vector.tensor_copy(h2[mt][:, HV:V], bank_b[mt][:])
        gates(0)
        gates(1)
        pick(2)
        gates(2)
        pick(3)
        gates(3)
        pick_times_gate(0, 0)
        pick_times_gate(0, 1)
        take_rest(0)
        pick_times_gate(1, 0)
        finish(0)
        pick_times_gate(1, 1)
        take_rest(1)
        take_diff(2)
        finish(1)
        weigh(2, slice(0, V))
        take_diff(3)
        add_back(2, slice(0, V))
        store(2)
        for hf in range(2):
            weigh(3, half(hf)[0])
        for hf in range(2):
            cols = half(hf)[0]
            add_back(3, cols)
            nc.sync.dma_start(out[3 * P : 4 * P, cols], res[3][:, cols])
